import numpy as np, ml_dtypes
CORES = [66,74,82,90,194,202,210,218]
N = 8
import mx_ref
BF = ml_dtypes.bfloat16
def gcols(t, e):
    v = np.concatenate([t.reshape(8, 16, -1, 4), np.zeros((8, 16, 1, 4), BF)], axis=2)
    return np.ascontiguousarray(np.stack([v[g][:, e[g]] for g in range(8)])).reshape(128, -1)
def tile(rs):
    return np.stack(rs, axis=2).reshape(128, -1).astype(BF)
def pick(q, e):
    c = np.concatenate([q[0].reshape(128, -1, 4), np.zeros((128, 1, 4), np.uint8)], axis=1); s = np.concatenate([q[1], np.ones((16, 1), np.uint8)], axis=1)
    return (np.ascontiguousarray(c[:, e].reshape(128, -1)), np.ascontiguousarray(s[:, e]))
def join(*qs):
    return (np.concatenate([q[0] for q in qs], axis=1), np.concatenate([q[1] for q in qs], axis=1))
def put(q, e, v):
    c, s = q[0].reshape(128, -1, 4).copy(), q[1].copy(); c[:, e] = v[0].reshape(128, -1, 4); s[:, e] = v[1]
    return (c.reshape(128, -1), s)
def pk(c, s):
    return (np.ascontiguousarray(c), mx_ref.live(s))
def emit(q):
    return q[0], q[1]
def packed(v, rng):
    q = [mx_ref.quantize(np.ascontiguousarray(v[r])) for r in range(N)]
    return np.stack([a for a, b in q]), np.stack([mx_ref.plane(b, rng) for a, b in q])
def values_of_codes():
    e, c = np.zeros((128, 128, 4), np.float32), np.zeros((128, 2, 4), np.uint8)
    e[np.arange(128), np.arange(128), 0] = 1
    c[:127, :, 0] = np.arange(256).reshape(2, 128).T[:127]
    return mx_ref.matmul(mx_ref.quantize(e.reshape(128, 512).astype(BF)), (c.reshape(128, 8), np.full((16, 2), 127, np.uint8))).T.reshape(-1).astype(np.float64)
CODE_VALUE, SCALE_VALUE = values_of_codes(), 2.0 ** (np.arange(256) - 127.0)
def decode(q):
    return (CODE_VALUE[q[0]].reshape(16, 8, -1, 4) * SCALE_VALUE[q[1]][:, None, :, None] + 0.0).reshape(128, -1).astype(np.float32)
def f(rng, *shape):
    return mx_ref.flush((rng.standard_normal(shape, dtype=np.float32) * np.exp2(rng.integers(-2, 3, shape[:-1] + (1,)))).astype(BF))
def wide(rng, *shape, cols=0):
    v = rng.standard_normal(shape, dtype=np.float32) * np.exp2(rng.integers(-12, 13, shape)).astype(np.float32)
    if cols: v *= np.repeat(np.exp2(rng.integers(-cols, cols + 1, shape[:-2] + (1, shape[-1] // 4))) * (rng.random(shape[:-2] + (1, shape[-1] // 4)) > 0.0625), 4, axis=-1).astype(np.float32)
    return mx_ref.flush(v.astype(BF))
C, H, B, P, R = 288, 144, 64, 3, 3
def addresses(s, c):
    key = np.sum((s > 0).reshape(8, 16, -1) * (1 << np.arange(16))[:, None], axis=1)
    return B * np.arange(3)[:, None] + ((key[:, None] * c.astype(np.int64)[:, None] >> 8) & (B - 1))
def written(d, a):
    left, peel, own = np.ones((8, H), bool), np.full((8, H), -1), np.zeros((8, H), int)
    for p in range(P):
        alone = np.zeros((8, 3, H), bool)
        for g in range(8): alone[g] = np.bincount(a[g][:, left[g]].reshape(-1), minlength=3 * B)[a[g]] == 1
        taken = left & alone.any(axis=1)
        peel[taken] = p
        own[taken] = np.argmax(alone, axis=1)[taken]
        left = left & ~taken
    cell, one, two = [np.take_along_axis(a, k[:, None], axis=1)[:, 0] for k in (own, np.where(own == 0, 1, 0), np.where(own == 2, 1, 2))]
    z = np.zeros((128, 12 * B), BF)
    for p in range(P - 1, -1, -1):
        n = ((d.astype(np.float32) - gcols(z, one).astype(np.float32)) - gcols(z, two).astype(np.float32)).astype(BF).reshape(8, 16, H, 4)
        w = z.reshape(8, 16, 3 * B, 4)
        for g in range(8): w[g][:, cell[g, peel[g] == p]] = n[g][:, peel[g] == p]
    return z
def big(v):
    v = v.astype(np.float32)
    v[np.abs(v) < np.float32(2.0 ** -16)] = 0
    return v.astype(BF)
def same(v):
    return np.repeat(v[None], N, axis=0)
def numbers_of(rng):
    return {"x": big(f(rng, N, 128, 4 * C)), "u": same(np.array(f(rng, 128, 512))), "v": np.array(f(rng, N, 128, 512))}
def weights(rng, still=0):
    w = big(f(rng, N, 128, 2048)).reshape(N, 8, 16, 4, 8, 16, 4)
    w[:, :, :, :, :, :still] = 0
    c, p = packed(w.reshape(N, 128, 2048), rng)
    return {"wc": c, "ws": p}
def factors(c):
    return {"hc": np.zeros((N, 128, 3), np.int32) + np.asarray(c).astype(np.int32)}
def odd(rng):
    return rng.permutation(128)[:3] * 2 + 1
def three(a, b):
    c = -a - b
    return np.array([[a, b, c], [b, c, a]]).reshape(2, -1)
def marked(rng, keys, size, k, fine=False):
    d = numbers_of(rng)
    x = d["x"].reshape(N, 8, 16, C, 4)
    x[:, :, :8] = 0
    u = np.zeros((128, 128, 4), np.float32)
    for i in range(16):
        m = np.where((keys >> i) & 1 == 1, 1, -rng.integers(0, 2, keys.shape)) * size
        x[:, :, i // 4, :, i % 4] = (m * np.where(fine, -1.25, 1.0) + 0.0).astype(np.float32).astype(BF)
        x[:, :, 4 + i // 4, :, i % 4] = (m * np.where(fine, 1.125, 0.0) + 0.0).astype(np.float32).astype(BF)
        for h in range(0, 128, 16):
            u[h + i // 4, h + i, i % 4] = k
            u[h + 4 + i // 4, h + i, i % 4] = 1.125 * k
    return {"x": x.reshape(N, 128, 4 * C), "u": same(u.reshape(128, 512).astype(BF)), "v": d["v"], **weights(rng, 8)}
def setup_inputs(rng):
    return {**numbers_of(rng), **weights(rng), **factors(odd(rng))}
def setup_inputs_near(rng):
    size = np.where(rng.permutation(N) < N // 2, 2.0 ** -30, 1.0)
    return {**marked(rng, rng.integers(0, 65536, (N, 8, C)), size[:, None, None], 2.0 ** -30), **factors(odd(rng))}
def setup_inputs_loads(rng):
    keys = rng.integers(0, 65536, (N, 8, C))
    size, fine = np.ones((N, 8, C)), np.zeros((N, 8, C), bool)
    n, last, j, cell = np.arange(H), np.full(H, B - 1), np.arange(28), np.arange(64)
    y = cell[cell % 8 > 0]
    q = y[y < 57]
    own = np.concatenate([[cell[8:], -cell[8:] & 56], [-y & 7, y], [q & 7, q & 56]], axis=1)
    second = np.concatenate([three(9 + 2 * j[:14], 37 + 2 * j[:14]), three(j // 4 * 8, j % 4 * 2 + 1), [[8, 4], [0, 4]]], axis=1)
    deep = np.concatenate([three(6 - 4 * j[:6], -18 - 4 * j[:6]), three(17 + 2 * j[:12], 41 + 2 * j[:12]), three(j[:24] // 4 * 8, j[:24] % 4 * 2 + 1)], axis=1)
    chains = [np.pad(k, ((0, 0), (0, H - k.shape[1]))) for k in (second, deep)]
    sign = np.concatenate([np.tile([1, 1, 1, -1, -1, -1], 3), np.tile([1, 1, 1, 0, 0, 0, 0, 0, 0, -1, -1, -1], 3), np.zeros(H - 54, int)])
    large = (6 - 4 * np.array([0, 1, 2, 9, 10, 11])) & 63
    asks = np.array([(s[i], s[k]) for s in ((6, -34, 28), (2, -30, 28), (2, -38, 36), (-2, -34, 36)) for i in range(3) for k in range(3) if i != k]).T
    first = [rng.permutation(8) for r in range(N)]
    shift = rng.integers(0, 64, (N, 2, 2, 2, 1))
    spot = []
    for r in range(N):
        for h in range(2):
            lo = H * h
            m = np.where(n < 128, n, rng.integers(10, 51, H))
            l = m.copy()
            l[0] = rng.integers(10, 51)
            s = last.copy()
            s[0] = 5
            o = first[r]
            if h == 1:
                e = first[r - 1][[2, 5, 6]]
                o = np.zeros(8, int)
                o[[3, 4, 7]] = e
                o[[0, 1, 2, 5, 6]] = rng.permutation(np.setdiff1d(np.arange(8), e))
            most = own[:, rng.permutation(161)[:H]]
            for i, (a, b) in enumerate([(last, last), (s, last), most, ((m + 1) // 2, m // 2), ((l + 1) // 2, l // 2)] + [chains[k] + shift[r, h, k] for k in range(2)]):
                e = rng.permutation(H)
                keys[r, o[i], lo + e] = ((a & 63) << 8) + ((b & 63) << 2) + (rng.integers(0, 4, H) << 14)
            fine[r, o[2], lo:lo + H] = True
            size[r, o[2], lo:lo + H] = 2.0 ** -30
            if h == 0: spot.append(e)
            if h == 1:
                k = keys[r, o[7], H:].copy()
                p, t = shift[r - 1, 0, 1]
                hit = np.isin(((k >> 8) - p) & 63, large) | np.isin(((k >> 2) - t) & 63, large) | np.isin((p + t - (k * 65 >> 8)) & 63, large)
                hit[rng.permutation(H)[:24]] = True
                i = np.flatnonzero(hit)
                a, b = asks[:, np.arange(len(i)) % 24]
                keys[r, o[7], H + i] = (((a + p) & 63) << 8) + (((b + t) & 63) << 2) + (rng.integers(0, 4, len(i)) << 14)
    d = marked(rng, keys, size, 2.0 ** -30, fine)
    x = d["x"].reshape(N, 8, 16, C, 4)
    i = np.flatnonzero(sign)
    for r in range(N):
        v = rng.choice([-1.0, 1.0], (8, 1, 4)) * 2.0 ** 28
        x[r, first[r][6], 8:][:, spot[r][i]] = (v * sign[i][:, None]).astype(np.float32).astype(BF)
    return {"x": x.reshape(N, 128, 4 * C), "u": d["u"], "v": d["v"], "wc": d["wc"], "ws": d["ws"], **factors(rng.permutation([1, 64, 65]))}
def setup_inputs_huge(rng):
    d = numbers_of(rng)
    x = rng.choice([-1.0, 1.0], (N, 128, C, 4)) * (0.6 + 0.2 * rng.random((N, 128, C, 4))) * 2.0 ** 24
    u = rng.choice([-1.0, 1.0], (128, 128, 4)) * (0.75 + 0.25 * rng.random((128, 128, 4))) * 2.0 ** 30
    for r in range(N):
        for lo in (0, H):
            e = lo + rng.permutation(H)
            for i in range(16): x[r][:, e[2 * i:2 * i + 2]] = (u[:, rng.integers(128)] * (0.5 if i % 2 else -0.5))[:, None]
    w = np.zeros((N, 128, 4, 128, 4), np.float32)
    i = np.arange(128)
    for b in range(4): w[:, i, b, i, b] = 1
    c, p = packed(w.reshape(N, 128, 2048).astype(BF), rng)
    return {"x": x.astype(np.float32).reshape(N, 128, 4 * C).astype(BF), "u": same(u.astype(np.float32).reshape(128, 512).astype(BF)), "v": d["v"], "wc": c, "ws": p, **factors(odd(rng))}
def setup_inputs_copies(rng):
    d = numbers_of(rng)
    x = d["x"].reshape(N, 128, C, 4)
    s, o = int(rng.integers(N)), rng.permutation(N)
    for r in range(N):
        for h in range(2):
            if r == s and h == 0: continue
            i = H * h + rng.permutation(H)[:[2, 16, H // 2, H][(o[r] + h) % 4]]
            x[r][:, i] = x[r][:, i[:1]]
    x[(s + 1) % N, :, H:] = x[s, :, :H]
    x[(s + 2) % N, :, :H] = 0
    x[(s + 3) % N, :, H:] = 0
    return {"x": x.reshape(N, 128, 4 * C), "u": d["u"], "v": d["v"], **weights(rng), **factors(odd(rng))}
def setup_inputs_spread(rng):
    d = setup_inputs(rng)
    d["x"] = big(wide(rng, N, 128, 4 * C, cols=6))
    d["hc"] = factors(rng.integers(1, 256, 3))["hc"]
    return d
def check_inputs(d):
    b = []
    for k in ("x", "u", "v"):
        a = np.abs(d[k].astype(np.float32))
        if not (np.isfinite(a).all() and ((a == 0) | (a >= 2.0 ** -30) & (a <= 2.0 ** 30)).all()): b.append("a value of " + k)
    if (d["u"] != d["u"][:1]).any(): b.append("u: not the same on all ranks")
    if (d["hc"] != d["hc"][:1, :1]).any(): b.append("hc: not the same in all rows and on all ranks")
    if ((d["hc"] < 1) | (d["hc"] > 255)).any(): b.append("hc: out of range")
    none, least, most = [emit(mx_ref.quantize(np.full((128, 16), k, np.float32).astype(BF)))[1][0, 0] for k in (0.0, 2.0 ** -30, 2.0 ** 30)]
    for r in range(N):
        if ((d["wc"][r] == 0x7F) | (d["wc"][r] == 0xFF)).any(): b.append("wc: a code that is no number")
        s = mx_ref.live(d["ws"][r])
        if ((s != none) & ((s < least) | (s > most))).any(): b.append("ws: a scale out of range")
        c = d["wc"][r].reshape(128, -1, 4)
        if ((c != 0) & (c != 0x80) & np.repeat(s == none, 8, axis=0)[:, :, None]).any(): b.append("wc: a number under the scale of zeros")
    return b
def reference(x, u, v, wc, ws, hc):
    qu = [mx_ref.quantize(u[r]) for r in range(N)]
    lay = [pk(wc[r], ws[r]) for r in range(N)]
    now = [x[r] for r in range(N)]
    for t in range(R):
        w = H * (t % 2)
        o = H - w
        num, adr, came = [], [], []
        for r in range(N):
            q = mx_ref.quantize(now[r])
            d = decode(q).astype(BF)
            a = addresses(mx_ref.matmul(qu[r], q), hc[r][0])
            z = written(np.ascontiguousarray(d[:, 4 * w:4 * w + 4 * H]), a[:, :, w:w + H])
            came.append(decode(mx_ref.quantize(z)).astype(BF))
            num.append(d)
            adr.append(a)
        for r in range(N):
            e = [gcols(came[(r - 1) % N], adr[r][:, k, o:o + H]).astype(np.float32) for k in range(3)]
            q = mx_ref.quantize(((e[0] + e[1]) + e[2]).astype(BF))
            new = now[r].copy()
            new[:, 4 * o:4 * o + 4 * H] = tile([mx_ref.matmul(pick(lay[r], np.arange(128 * b, 128 * b + 128)), q) * np.float32(0.015625) + num[r][:, 4 * o + b:4 * o + 4 * H:4].astype(np.float32) for b in range(4)])
            now[r] = new
    y = np.zeros((N, 128, C), np.float32)
    oc, osc = np.zeros((N, 128, 4 * C), np.uint8), np.zeros((N, 16, C), np.uint8)
    for r in range(N):
        q = mx_ref.quantize(now[r])
        y[r] = mx_ref.matmul(mx_ref.quantize(v[r]), q)
        oc[r], osc[r] = emit(q)
    return {"y": y, "oc": oc, "osc": osc}

@@ -1,0 +1,460 @@
+from concourse.mybir import dt, AluOpType as A, ActivationFunctionType as F, AxisListType as AX
+
+H = 144
+BIG = float(2 ** 20)
+CQ, BF, F32, I32, U16, U8 = "float8_e4m3fn_x4", "bfloat16", "float32", "int32", "uint16", "uint8"
+COLS = "pw bigp sc4 tm4 sc12 tm12 dsc nq thr".split()
+
+SCRATCH = {"ps": ("psum", [128, 4096], F32)}
+for _names, _n, _t in [
+    ("xa xb", 576, BF), ("ub vb", 512, BF), ("hci", 4, I32), ("hcf", 4, F32),
+    ("wq", 512, CQ), ("wsc", 512, U8), ("uq vq kwq boq", 128, CQ), ("us vs kws bos", 128, U8),
+    ("kw bo", 512, BF), ("eye", 516, BF), ("c64", 128, BF), ("eq", 512, CQ), ("es", 512, U8),
+    ("pidx", 1, I32), ("pint", 4, I32), ("pf", 4, F32), ("grp", 128, BF), ("jm c16a c16", H, F32), ("c32", 2 * H, F32),
+    ("jm4 sg4 c4", 480, BF), ("c3", 672, BF), ("d16", 16, F32), ("d4", 4, F32),
+    ("col", len(COLS), F32), ("cell", 192, BF), ("enc", 192, F32), ("dm0 dm", 9, F32), ("ids", H, BF),
+    ("bt", 576, BF), ("btq", H, CQ), ("bts", H, U8), ("ks", H, F32), ("xi hb li", 30, I32), ("hg hr", 30, F32),
+    ("ot", 2304, BF), ("otq", 576, CQ), ("ots", 576, U8), ("wn", 192, F32), ("g1", H, F32), ("g2 sp0 sp1 sp2", 2 * H, F32),
+    ("s01 s12 rm q9 z9 ac0 ac1", 9, F32), ("en", 9, I32), ("xy", 18, F32),
+    ("tw ew", 580, BF), ("tw2", 256, BF), ("iv", 960, BF), ("n3", 1740, BF), ("t1", 256, F32), ("t2 f1", 576, F32),
+    ("zt f0 ft xn", 576, BF), ("zq fq", H, CQ), ("zs fs", H, U8), ("ga gb", 2 * H, BF), ("oab oab3", 72, U16),
+    ("ra rb", 480, BF), ("ord", 120, U16), ("ya yb", H, F32),
+    ("xq0 xq1 xq2 xq3 xq4", H, CQ), ("xs0 xs1 xs2 xs3 xs4", H, U8),
+    ("ho0 ho1 ho2 ho3", 30, U16),
+    ("lq0 lq1 lq2", H, CQ), ("ls0 ls1 ls2", H, U8), ("ll0 ll1 ll2 sl0 sl1 sl2", 30, U16), ("ow0 ow1 ow2", 336, BF),
+]:
+    for _x in _names.split():
+        SCRATCH[_x] = ("sbuf", [128, _n], _t)
+
+SEMAPHORES = ["nV", "nS", "nP", "nG", "sent", "stY", "stS"] + ["ld%d" % i for i in range(8)] + \
+             ["ac%d" % i for i in range(3)] + ["al%d" % i for i in range(3)]
+
+
+def rank_program(g, core, T, topo):
+    rank = T.rank_of(core)
+    if rank is None:
+        return
+    nxt = T.cores[(rank + 1) % len(T.cores)]
+    rid, pid = topo.addr(nxt, core)
+    mask = topo.mask(core, nxt)
+    neng = len(topo.engines(core, nxt))
+    Q = {"V": g.vector, "S": g.scalar, "P": g.tensor, "G": g, "Y": g.sync}
+    ops = []
+
+    def v(name, a=0, b=None, s=1):
+        if name in COLS:
+            return ("col", COLS.index(name), COLS.index(name) + 1, 1)
+        return (name, a, SCRATCH[name][1][1] if b is None else b, s)
+
+    def ap(x):
+        if isinstance(x, tuple):
+            return T[x[0]][:, x[1]:x[2]] if x[3] == 1 else T[x[0]][:, x[1]:x[2]:x[3]]
+        return x
+
+    def bank(b, n):
+        return v("ps", 512 * b, 512 * b + n)
+
+    def add(q, fn, reads, writes, sem=None, inc=0):
+        ops.append({"q": q, "fn": fn, "r": [x for x in reads if isinstance(x, tuple)], "w": list(writes), "sem": sem, "inc": inc})
+
+    def src(x):
+        if isinstance(x, list):
+            return ap(x[1]).indirect(ap(x[2]))
+        return ap(x)
+
+    def rd(x):
+        return [x[1], x[2]] if isinstance(x, list) else [x]
+
+    def gat(win, off):
+        return ["gather", win, off]
+
+    def ts(out, in0, s1, s2, o0, o1=None):
+        if o1 is None:
+            add("V", lambda: g.vector.tensor_scalar(ap(out), src(in0), ap(s1), None, o0), rd(in0) + [s1], [out])
+        else:
+            add("V", lambda: g.vector.tensor_scalar(ap(out), src(in0), ap(s1), ap(s2), o0, o1), rd(in0) + [s1, s2], [out])
+
+    def tt(out, in0, in1, o):
+        add("V", lambda: g.vector.tensor_tensor(ap(out), src(in0), ap(in1), o), rd(in0) + [in1], [out])
+
+    def cp(out, in_):
+        add("V", lambda: g.vector.tensor_copy(ap(out), src(in_)), rd(in_), [out])
+
+    def scatter(win, off, in_):
+        add("V", lambda: g.vector.tensor_copy(ap(win).indirect(ap(off)), ap(in_)), [off, in_], [win])
+
+    def ms(out, c):
+        add("V", lambda: g.vector.memset(ap(out), c), [], [out])
+
+    def scan(out, d0, d1, o0, o1=A.max):
+        add("V", lambda: g.vector.tensor_tensor_scan(ap(out), ap(d0), ap(d1), 0.0, o0, o1), [d0, d1], [out])
+
+    def prod(out, in_):
+        add("V", lambda: g.vector.tensor_reduce(ap(out), ap(in_), AX.X, A.mult), [in_], [out])
+
+    def act(out, in_, f=F.Copy, scale=1.0, bias=None):
+        if bias is None:
+            add("S", lambda: g.scalar.activation(ap(out), src(in_), f, scale=ap(scale)), rd(in_) + [scale], [out])
+        else:
+            add("S", lambda: g.scalar.activation(ap(out), src(in_), f, bias=ap(bias), scale=ap(scale)), rd(in_) + [scale, bias], [out])
+
+    def quant(c, s, in_):
+        add("V", lambda: g.vector.quantize_mx(ap(c), ap(s), ap(in_)), [in_], [c, s])
+
+    def mm(out, lc, ls, rc, rs, start=True, stop=True):
+        add("P", lambda: g.tensor.matmul_mx(ap(out), ap(lc), ap(ls), ap(rc), ap(rs), start, stop), [lc, ls, rc, rs], [out])
+
+    def iota(out, pat, base, ch=0):
+        if SCRATCH[out[0]][2] == I32:
+            add("G", lambda: g.iota(ap(out), pat, base, ch), [], [out])
+        else:
+            add("G", lambda: g.iota(ap(out), pat, base, ch, allow_small_or_imprecise_dtypes=True), [], [out])
+
+    def fillg(out, c):
+        iota(out, [[0, len(range(out[1], out[2], out[3]))]], c)
+
+    def load(q, out, out_ap, in_ap, sem):
+        add(q, lambda: Q[q].dma_start(out_ap, in_ap), [], [out], sem, 16)
+
+    def store(q, out_ap, in_, in_ap):
+        add(q, lambda: Q[q].dma_start(out_ap, in_ap), [in_], [], "st" + q, 16)
+
+    def send(out_ap, in_, in_ap, sem):
+        add("G", lambda: g.remote_dma(out_ap, in_ap, T.sem[sem], T.sem.sent, pid, rid, mask), [in_], [], "sent", 0)
+
+    def arrive(outs, sem, n):
+        add(None, None, [], outs, sem, n)
+
+    def u8(name):
+        return T[name][:].bitcast(dt.uint8)
+
+    def xq(i):
+        return v("xq%d" % i), v("xs%d" % i)
+
+    def eb(b):
+        return v("eq", 128 * b, 128 * b + 128), v("es", 128 * b, 128 * b + 128)
+
+    pi, pg, pt, pq = v("pf", 0, 1), v("pf", 1, 2), v("pf", 2, 3), v("pf", 3, 4)
+    bigp, thr = v("bigp"), v("thr")
+
+    load("Y", v("xa"), T.xa[:], T.x[:, 0:576], "ld0")
+    load("S", v("ub"), T.ub[:], T.u[:], "ld1")
+    load("Y", v("xb"), T.xb[:], T.x[:, 576:1152], "ld3")
+    load("S", v("hci", 0, 3), T.hci[:, 0:3], T.hc[:], "ld2")
+    load("Y", v("wq"), u8("wq"), T.wc[:], "ld4")
+    load("Y", v("wsc"), T.wsc[:], T.ws[:], "ld5")
+    load("Y", v("vb"), T.vb[:], T.v[:], "ld6")
+    for t in range(3):
+        arrive([v("lq%d" % t), v("ls%d" % t)], "ac%d" % t, 2 * neng)
+        arrive([v("ll%d" % t)], "al%d" % t, neng)
+
+    iota(v("pidx"), [[0, 1]], 0, 1)
+    iota(v("jm"), [[0, 9], [1, 16]], 0)
+    iota(v("grp"), [[1, 8], [0, 16]], 0)
+    ms(v("c64"), 64.0)
+    ms(v("eye"), 0.0)
+    add("G", lambda: g.affine_select(ap(v("eye", 3, 515, 4)), ap(v("c64")), [[-1, 128]], A.is_equal, 0.0, 0, 1), [v("c64")], [v("eye", 3, 515, 4)])
+    iota(v("cell"), [[1, 192]], 0)
+    fillg(v("xi"), 0)
+    fillg(v("ot", 3, 2304, 4), 0)
+    ts(v("pint", 0, 1), v("pidx"), 15, None, A.bitwise_and)
+    ts(v("pint", 1, 2), v("pidx"), 4, None, A.logical_shift_right)
+    ts(v("pint", 2, 3), v("pidx"), 3, None, A.bitwise_and)
+    ts(v("pint", 3, 4), v("pidx"), 2, 3, A.logical_shift_right, A.bitwise_and)
+    ms(v("kw"), 0.0)
+    cp(v("pf"), v("pint"))
+    ms(v("bt"), 0.0)
+    ts(v("d16"), v("jm", 0, 16), pi, 1.0, A.is_lt, A.add)
+    ts(bigp, pi, -BIG, 15 * BIG, A.mult, A.add)
+    ts(v("c16a"), v("jm"), pi, 31.0 / 32, A.is_gt, A.subtract)
+    prod(v("pw"), v("d16"))
+    act(v("c16"), v("c16a"), scale=32 * BIG)
+    act(v("c32", 0, 2 * H, 2), v("c16a"), scale=32 * BIG)
+    act(v("c32", 1, 2 * H, 2), v("c16a"), scale=0.0)
+    ts(v("bo", 0, 512, 4), v("grp"), pg, 4096.0, A.is_equal, A.mult)
+    ts(v("kw", 0, 512, 4), v("grp"), pg, v("pw"), A.is_equal, A.mult)
+    for t in range(1, 4):
+        act(v("bo", t, 512, 4), v("bo", 0, 512, 4))
+    quant(*eb(0), v("eye", 3, 515))
+    quant(v("kwq"), v("kws"), v("kw"))
+    for b in range(1, 4):
+        quant(*eb(b), v("eye", 3 - b, 515 - b))
+    quant(*xq(0), v("xa"))
+    quant(v("uq"), v("us"), v("ub"))
+
+    def setup_b():
+        quant(*xq(1), v("xb"))
+        cp(v("hcf", 0, 3), v("hci", 0, 3))
+
+    def setup_c():
+        quant(v("boq"), v("bos"), v("bo"))
+        ts(thr, pi, -BIG, -BIG, A.mult, A.add)
+        ts(v("dsc"), pi, 1 - BIG, -BIG, A.mult, A.add)
+
+    def setup_g():
+        iota(v("enc"), [[64 - 1024, 3], [1, 64]], 3072 + 4096 - 2 ** 24)
+        iota(v("dm0"), [[16, 9]], 192)
+        fillg(v("li"), 0)
+        iota(v("jm4"), [[0, 120], [1, 4]], 0)
+        iota(v("ids"), [[4, H]], 4)
+        fillg(v("ow0"), 580)
+        fillg(v("tw", 576, 580), 0)
+        fillg(v("ew", 576, 580), 0)
+        fillg(v("n3", 1728, 1740), 0)
+        fillg(v("n3", 0, 768), 0)
+        fillg(v("c3", 0, 672, 3), 0)
+
+    def setup_f():
+        ts(v("nq"), pq, -1.0, -0.5, A.mult, A.add)
+        ts(v("d4"), v("jm4", 0, 4), pq, 2.0 ** -8, A.is_le, A.max)
+        ts(v("tm4"), pt, -4.0, None, A.add)
+        ts(v("tm12"), pt, 3.0, -10.0, A.mult, A.add)
+        prod(v("sc4"), v("d4"))
+        act(v("sg4"), v("jm4"), F.Sign, bias=v("nq"))
+        ms(v("c3", 1, 672, 3), 1.0)
+        ms(v("c3", 2, 672, 3), 1.0)
+        ts(v("sc12"), v("sc4"), 3.0, None, A.mult)
+
+    def keys(xi_, hg, fill1=None, fill2=None):
+        mm(bank(4, H), v("uq"), v("us"), *xq(xi_))
+        if fill1:
+            fill1()
+        ts(v("bt", 0, 576, 4), bank(4, H), 0.0, None, A.is_gt)
+        quant(v("btq"), v("bts"), v("bt"))
+        mm(bank(5, H), v("kwq"), v("kws"), v("btq"), v("bts"))
+        if fill2:
+            fill2()
+        scan(v("ks"), v("c16"), bank(5, H), A.add)
+        for k in range(3):
+            ts(v("xi", 10 * k, 10 * k + 9), v("ks", 15, H, 16), bigp, v("hcf", k, k + 1), A.subtract, A.mult)
+        ts(v("hb"), v("xi"), 8, 63, A.logical_shift_right, A.bitwise_and)
+        for k in range(3):
+            ts(v(hg, 10 * k, 10 * k + 10), v("hb", 10 * k, 10 * k + 10), 64.0 * k, None, A.add)
+
+    def hcol(k, m):
+        return v("hg", 10 * k + m, 10 * k + m + 1)
+
+    def hlist(k):
+        return v("hg", 10 * k, 10 * k + 9)
+
+    def count(j):
+        c, s = v("otq", 192 * j, 192 * j + 192), v("ots", 192 * j, 192 * j + 192)
+        quant(c, s, v("ot", 768 * j, 768 * j + 768))
+        mm(bank(6, 192), v("boq"), v("bos"), c, s, j == 0, j == 2)
+
+    def peel(t, p, fill):
+        ho = "ho%d" % t
+        if p == 0:
+            for m in (7, 8):
+                for k in range(3):
+                    a = 768 * 2 + 256 * k + m - 6
+                    act(v("ot", a, a + 253, 4), v("cell", 64 * k, 64 * k + 64), F.Abs, scale=-1.0, bias=hcol(k, m))
+            for m in (7, 8):
+                o = v("ot", 768 * 2 + m - 6, 2304, 4)
+                act(o, o, F.Relu, scale=-1.0, bias=1.0)
+            for m in range(7):
+                for k in range(3):
+                    a = 768 * (m // 3) + 256 * k + m % 3
+                    ts(v("ot", a, a + 253, 4), v("cell", 64 * k, 64 * k + 64), hcol(k, m), None, A.is_equal)
+                if m == 3:
+                    count(0)
+            count(1)
+            count(2)
+        else:
+            for m in range(6, 9):
+                o = v("ot", 768 * 2 + m - 6, 2304, 4)
+                act(o, o, F.Identity, scale=v("rm", m, m + 1))
+            for m in range(6):
+                o = v("ot", 768 * (m // 3) + m % 3, 768 * (m // 3) + 768, 4)
+                ts(o, o, v("sp%d" % (p - 1), 32 * m + 31, 32 * m + 32), thr, A.mult, A.is_lt)
+            count(0)
+            count(1)
+            count(2)
+        fill()
+        tt(v("wn"), v("enc"), bank(6, 192), A.subtract)
+        act(v("g2", 0, 2 * H, 2), gat(v("wn"), v(ho, 0, 9)))
+        cp(v("g1"), gat(v("wn"), v(ho, 10, 19)))
+        tt(v("g2", 1, 2 * H, 2), gat(v("wn"), v(ho, 20, 29)), v("g1"), A.max)
+        scan(v("sp%d" % p), v("c32"), v("g2"), A.add)
+        if p < 2:
+            ts(v("rm"), v("sp%d" % p, 31, 2 * H, 32), thr, None, A.is_lt)
+
+    def keep(p):
+        a = v("sp%d" % p, 31, 2 * H, 32)
+        ts(v("q9"), a, thr, 16384.0 / (p + 1), A.is_gt, A.mult)
+        if p == 0:
+            ts(v("dm"), v("dm0"), v("dsc"), None, A.add)
+        tt(v("z9"), v("q9"), a, A.add)
+        tt(v("ac%d" % p), v("z9"), v("dm") if p == 0 else v("ac0"), A.max)
+
+    def finish_half(i, lo, ybuf, b):
+        mm(bank(b, H), v("vq"), v("vs"), *xq(i))
+        store("Y", T.oc[:, 4 * lo:4 * lo + 4 * H], v("xq%d" % i), u8("xq%d" % i))
+        for k in range(4):
+            store("S" if i == 4 else "Y", T.osc[4 * k:4 * k + 4, lo:lo + H], v("xs%d" % i), T["xs%d" % i][32 * k:32 * k + 4, :])
+        if i == 4:
+            cp(v(ybuf), bank(b, H))
+        else:
+            act(v(ybuf), bank(b, H))
+        store("Y", T.y[:, lo:lo + H], v(ybuf), T[ybuf][:])
+
+    writers, readers, rlist = [0, 2, 3], [1, 0, 2], ["ho3", "ho0", "ho1"]
+    for t in range(3):
+        w = writers[t]
+        send(u8("lq%d" % t), v("xq%d" % w), u8("xq%d" % w), "ac%d" % t)
+        send(T["ls%d" % t][:], v("xs%d" % w), T["xs%d" % w][:], "ac%d" % t)
+        if t == 0:
+            setup_g()
+            keys(w, "hg", setup_b, setup_c)
+        else:
+            fillg(v("ow%d" % t), 580)
+            keys(w, "hg")
+
+        def fill0():
+            cp(v("ho%d" % t), v("hg"))
+            tt(v("s01"), hlist(0), hlist(1), A.add)
+            tt(v("s12"), hlist(1), hlist(2), A.add)
+
+        peel(t, 0, fill0)
+        peel(t, 1, lambda: keep(0))
+        peel(t, 2, lambda: keep(1))
+        tt(v("en"), v("sp2", 31, 2 * H, 32), v("ac1"), A.max)
+        ts(v("li", 0, 9), v("en"), 1023, None, A.bitwise_and)
+        tt(v("xy", 0, 9), v("s01"), v("li", 0, 9), A.subtract)
+        tt(v("xy", 9, 18), v("s12"), v("li", 0, 9), A.subtract)
+        tt(v("li", 10, 19), v("xy", 0, 9), hlist(0), A.max)
+        tt(v("li", 20, 29), v("xy", 9, 18), hlist(2), A.min)
+        cp(v("sl%d" % t), v("li"))
+        send(T["ll%d" % t][:], v("sl%d" % t), T["sl%d" % t][:], "al%d" % t)
+
+        for b in range(4):
+            mm(bank(b, H), *eb(b), v("lq%d" % t), v("ls%d" % t))
+        for b in range(4):
+            act(v("tw", b, 576, 4), bank(b, H), scale=2.0 ** -6)
+        act(v("tw2"), v("tw", 0, 256))
+        act(v("iv", 0, 960, 3), v("tw", 256, 576), scale=-1.0)
+        if t == 0:
+            keys(1, "hr", setup_f)
+            act(v("c4"), v("sg4"), scale=256.0)
+            cp(v("ho3"), v("hr"))
+        if t == 1:
+            quant(v("vq"), v("vs"), v("vb"))
+        if t == 2:
+            finish_half(3, 0, "ya", 7)
+        for b in range(4):
+            mm(bank(b, H), *eb(b), *xq(readers[t]), True, False)
+
+        ll, ow = "ll%d" % t, "ow%d" % t
+        scatter(v(ow), v(ll, 0, 9), v("ids"))
+        act(v("ga", H, 2 * H), gat(v(ow, 0, 192), v(ll, 20, 29)))
+        cp(v("ga", 0, H), gat(v(ow, 0, 192), v(ll, 10, 19)))
+        scan(v("gb"), v("c4", 0, 2 * H), v("ga"), A.mult)
+        ts(v("oab"), v("gb", 3, 2 * H, 4), v("sc4"), v("tm4"), A.mult, A.add)
+        for a, b in ((16, 30), (30, 36)):
+            for s in range(2):
+                act(v("iv", 48 * (a - 16) + 1 + s, 48 * (b - 16), 3), gat(v("tw"), v("oab", 36 * s + a, 36 * s + b)))
+        act(v("ra"), gat(v(ow, 0, 192), v(rlist[t])))
+        tt(v("t1"), gat(v("tw"), v("oab", 0, 16)), v("tw2"), A.subtract)
+        ts(v("oab3"), v("gb", 3, 2 * H, 4), v("sc12"), v("tm12"), A.mult, A.add)
+        tt(v("n3", 2, 768, 3), gat(v("tw"), v("oab", 36, 52)), v("t1"), A.add)
+        scan(v("n3", 768, 1440), v("c3"), v("iv", 0, 672), A.mult, A.add)
+        scan(v("n3", 1440, 1728), v("c3", 0, 288), v("iv", 672, 960), A.mult, A.add)
+        tt(v("t2"), gat(v("n3"), v("oab3", 0, 36)), v("tw", 0, 576), A.add)
+        tt(v("zt"), gat(v("n3"), v("oab3", 36, 72)), v("t2"), A.add)
+        quant(v("zq"), v("zs"), v("zt"))
+        for b in range(4):
+            mm(bank(4 + b, H), *eb(b), v("zq"), v("zs"))
+        scan(v("rb"), v("c4"), v("ra"), A.mult)
+        ts(v("ord"), v("rb", 3, 480, 4), v("sc4"), v("tm4"), A.mult, A.add)
+        for b in range(4):
+            if b % 2 == 0:
+                act(v("ew", b, 576, 4), bank(4 + b, H), scale=2.0 ** -6)
+            else:
+                ts(v("ew", b, 576, 4), bank(4 + b, H), 2.0 ** -6, None, A.mult)
+        act(v("f0", 192, 576), gat(v("ew"), v("ord", 12, 36)))
+        cp(v("f0", 0, 192), gat(v("ew"), v("ord", 0, 12)))
+        tt(v("f1", 0, 192), gat(v("ew"), v("ord", 40, 52)), v("f0", 0, 192), A.add)
+        tt(v("f1", 192, 576), gat(v("ew"), v("ord", 52, 76)), v("f0", 192, 576), A.add)
+        tt(v("ft"), gat(v("ew"), v("ord", 80, 116)), v("f1"), A.add)
+        quant(v("fq"), v("fs"), v("ft"))
+        for b in range(4):
+            mm(bank(b, H), v("wq", 128 * b, 128 * b + 128), v("wsc", 128 * b, 128 * b + 128), v("fq"), v("fs"), False, True)
+        for b in range(4):
+            if b % 2 == 0:
+                act(v("xn", b, 576, 4), bank(b, H), scale=2.0 ** -6)
+            else:
+                ts(v("xn", b, 576, 4), bank(b, H), 2.0 ** -6, None, A.mult)
+        quant(*xq(2 + t), v("xn"))
+    finish_half(4, H, "yb", 7)
+
+    def cols(x):
+        if x[0] == "ps":
+            return {x[1] // 512}
+        return set(range(x[1], x[2], x[3]))
+
+    seen = {}
+    clock = {q: {} for q in Q}
+    seq = {q: 0 for q in Q}
+    for i, o in enumerate(ops):
+        q = o["q"]
+        deps = set()
+        acc = [(x[0], cols(x), False) for x in o["r"]] + [(x[0], cols(x), True) for x in o["w"]]
+        for name, cs, wr in acc:
+            for j, cj, wj in seen.get(name, []):
+                qj = ops[j]["q"]
+                if name == "ps":
+                    if qj == q and (q == "P" or not (wr or wj)):
+                        continue
+                elif not (wr or wj):
+                    continue
+                if cs & cj:
+                    deps.add(j)
+        for name, cs, wr in acc:
+            seen.setdefault(name, []).append((i, cs, wr))
+        if o["sem"] is None:
+            seq[q] += 1
+            o["key"], o["pos"] = q, seq[q]
+        else:
+            o["key"], o["pos"] = ("a", i), 1
+        o["waits"] = []
+        if q is not None:
+            ck = clock[q]
+            for j in sorted(deps, reverse=True):
+                d = ops[j]
+                if ck.get(d["key"], 0) >= d["pos"]:
+                    continue
+                o["waits"].append(j)
+                d["sig"] = True
+                for kk, vv in d["clock"].items():
+                    if ck.get(kk, 0) < vv:
+                        ck[kk] = vv
+                ck[d["key"]] = max(ck.get(d["key"], 0), d["pos"])
+            o["clock"] = dict(ck)
+        else:
+            o["clock"] = {}
+    n = {q: 0 for q in Q}
+    total = {}
+    for o in ops:
+        if o["sem"] is None:
+            if o.get("sig"):
+                n[o["q"]] += 1
+                o["val"] = n[o["q"]]
+        else:
+            o["val"] = o["inc"]
+    for o in ops:
+        q = o["q"]
+        if q is None:
+            continue
+        for j in o["waits"]:
+            d = ops[j]
+            Q[q].wait_ge(T.sem[d["sem"] or "n" + d["q"]], d["val"])
+        ins = o["fn"]()
+        if o["sem"] is None:
+            if o.get("sig"):
+                ins.then_inc(T.sem["n" + q], 1)
+        elif o["inc"]:
+            ins.then_inc(T.sem[o["sem"]], o["inc"])
+            total[o["sem"]] = total.get(o["sem"], 0) + o["inc"]
+    g.wait_ge(T.sem.sent, 9 * neng)
+    g.sync.wait_ge(T.sem.stY, total["stY"])
+    g.scalar.wait_ge(T.sem.stS, total["stS"])

@@ -10,11 +10,11 @@ for _names, _n, _t in [
     ("xa xb", 576, BF), ("ub vb", 512, BF), ("hci", 4, I32), ("hcf", 4, F32),
     ("wq", 512, CQ), ("wsc", 512, U8), ("uq vq kwq boq", 128, CQ), ("us vs kws bos", 128, U8),
     ("kw bo", 512, BF), ("eye", 516, BF), ("c64", 128, BF), ("eq", 512, CQ), ("es", 512, U8),
-    ("pidx", 1, I32), ("pint", 4, I32), ("pf", 4, F32), ("grp", 128, BF), ("jm c16a c16", H, F32), ("c32", 2 * H, F32),
+    ("pidx", 1, I32), ("pint", 4, I32), ("pf", 4, F32), ("grp", 128, BF), ("jm c16a c16", H, F32), ("c48", 3 * H, F32),
     ("jm4 sg4 c4", 480, BF), ("c3", 672, BF), ("d16", 16, F32), ("d4", 4, F32),
     ("col", len(COLS), F32), ("cell", 192, BF), ("enc", 192, F32), ("dm0 dm", 9, F32), ("ids", H, BF),
     ("bt", 576, BF), ("btq", H, CQ), ("bts", H, U8), ("ks", H, F32), ("xi hb li", 30, I32), ("hg hr", 30, F32),
-    ("ot", 2304, BF), ("otq", 576, CQ), ("ots", 576, U8), ("wn", 192, F32), ("g1", H, F32), ("g2 sp0 sp1 sp2", 2 * H, F32),
+    ("ot", 2304, BF), ("otq", 576, CQ), ("ots", 576, U8), ("wn", 192, F32), ("g3 sp0 sp1 sp2", 3 * H, F32),
     ("s01 s12 rm q9 z9 ac0 ac1", 9, F32), ("en", 9, I32), ("xy", 18, F32),
     ("tw ew", 580, BF), ("tw2", 256, BF), ("iv", 960, BF), ("n3", 1740, BF), ("t1", 256, F32), ("t2 f1", 576, F32),
     ("zt f0 ft xn", 576, BF), ("zq fq", H, CQ), ("zs fs", H, U8), ("ga gb", 2 * H, BF), ("oab oab3", 72, U16),
@@ -167,18 +167,20 @@ def rank_program(g, core, T, topo):
     ts(v("d16"), v("jm", 0, 16), pi, 1.0, A.is_lt, A.add)
     ts(bigp, pi, -BIG, 15 * BIG, A.mult, A.add)
     ts(v("c16a"), v("jm"), pi, 31.0 / 32, A.is_gt, A.subtract)
+    ts(v("bo", 0, 512, 4), v("grp"), pg, 4096.0, A.is_equal, A.mult)
     prod(v("pw"), v("d16"))
     act(v("c16"), v("c16a"), scale=32 * BIG)
-    act(v("c32", 0, 2 * H, 2), v("c16a"), scale=32 * BIG)
-    act(v("c32", 1, 2 * H, 2), v("c16a"), scale=0.0)
-    ts(v("bo", 0, 512, 4), v("grp"), pg, 4096.0, A.is_equal, A.mult)
-    ts(v("kw", 0, 512, 4), v("grp"), pg, v("pw"), A.is_equal, A.mult)
     for t in range(1, 4):
         act(v("bo", t, 512, 4), v("bo", 0, 512, 4))
+    act(v("c48", 0, 3 * H, 3), v("c16a"), scale=32 * BIG)
+    act(v("c48", 1, 3 * H, 3), v("c16a"), scale=0.0)
+    act(v("c48", 2, 3 * H, 3), v("c16a"), scale=0.0)
     quant(*eb(0), v("eye", 3, 515))
+    quant(*eb(1), v("eye", 2, 514))
+    ts(v("kw", 0, 512, 4), v("grp"), pg, v("pw"), A.is_equal, A.mult)
+    quant(*eb(2), v("eye", 1, 513))
+    quant(*eb(3), v("eye", 0, 512))
     quant(v("kwq"), v("kws"), v("kw"))
-    for b in range(1, 4):
-        quant(*eb(b), v("eye", 3 - b, 515 - b))
     quant(*xq(0), v("xa"))
     quant(v("uq"), v("us"), v("ub"))
 
@@ -209,11 +211,10 @@ def rank_program(g, core, T, topo):
         ts(v("d4"), v("jm4", 0, 4), pq, 2.0 ** -8, A.is_le, A.max)
         ts(v("tm4"), pt, -4.0, None, A.add)
         ts(v("tm12"), pt, 3.0, -10.0, A.mult, A.add)
+        ms(v("c3", 1, 672, 3), 1.0)
         prod(v("sc4"), v("d4"))
         act(v("sg4"), v("jm4"), F.Sign, bias=v("nq"))
-        ms(v("c3", 1, 672, 3), 1.0)
         ms(v("c3", 2, 672, 3), 1.0)
-        ts(v("sc12"), v("sc4"), 3.0, None, A.mult)
 
     def keys(xi_, hg, fill1=None, fill2=None):
         mm(bank(4, H), v("uq"), v("us"), *xq(xi_))
@@ -227,7 +228,8 @@ def rank_program(g, core, T, topo):
         scan(v("ks"), v("c16"), bank(5, H), A.add)
         for k in range(3):
             ts(v("xi", 10 * k, 10 * k + 9), v("ks", 15, H, 16), bigp, v("hcf", k, k + 1), A.subtract, A.mult)
-        ts(v("hb"), v("xi"), 8, 63, A.logical_shift_right, A.bitwise_and)
+        for k in range(3):
+            ts(v("hb", 10 * k, 10 * k + 10), v("xi", 10 * k, 10 * k + 10), 8, 63, A.logical_shift_right, A.bitwise_and)
         for k in range(3):
             ts(v(hg, 10 * k, 10 * k + 10), v("hb", 10 * k, 10 * k + 10), 64.0 * k, None, A.add)
 
@@ -237,50 +239,47 @@ def rank_program(g, core, T, topo):
     def hlist(k):
         return v("hg", 10 * k, 10 * k + 9)
 
-    def count(j):
+    def count(j, first, last):
         c, s = v("otq", 192 * j, 192 * j + 192), v("ots", 192 * j, 192 * j + 192)
         quant(c, s, v("ot", 768 * j, 768 * j + 768))
-        mm(bank(6, 192), v("boq"), v("bos"), c, s, j == 0, j == 2)
+        mm(bank(6, 192), v("boq"), v("bos"), c, s, first, last)
+
+    def hot(m, k=None):
+        a = 768 * (m // 3) + m % 3
+        return v("ot", a, 768 * (m // 3) + 768, 4) if k is None else v("ot", a + 256 * k, a + 256 * k + 253, 4)
 
     def peel(t, p, fill):
-        ho = "ho%d" % t
+        ho, sp = "ho%d" % t, "sp%d" % p
         if p == 0:
-            for m in (7, 8):
+            for k in range(3):
+                for m in range(3):
+                    act(hot(m, k), v("cell", 64 * k, 64 * k + 64), F.Abs, scale=-1.0, bias=hcol(k, m))
+            for m in range(3):
+                act(hot(m), hot(m), F.Relu, scale=-1.0, bias=1.0)
+            for j in (1, 2):
                 for k in range(3):
-                    a = 768 * 2 + 256 * k + m - 6
-                    act(v("ot", a, a + 253, 4), v("cell", 64 * k, 64 * k + 64), F.Abs, scale=-1.0, bias=hcol(k, m))
-            for m in (7, 8):
-                o = v("ot", 768 * 2 + m - 6, 2304, 4)
-                act(o, o, F.Relu, scale=-1.0, bias=1.0)
-            for m in range(7):
-                for k in range(3):
-                    a = 768 * (m // 3) + 256 * k + m % 3
-                    ts(v("ot", a, a + 253, 4), v("cell", 64 * k, 64 * k + 64), hcol(k, m), None, A.is_equal)
-                if m == 3:
-                    count(0)
-            count(1)
-            count(2)
+                    for m in range(3 * j, 3 * j + 3):
+                        ts(hot(m, k), v("cell", 64 * k, 64 * k + 64), hcol(k, m), None, A.is_equal)
         else:
-            for m in range(6, 9):
-                o = v("ot", 768 * 2 + m - 6, 2304, 4)
-                act(o, o, F.Identity, scale=v("rm", m, m + 1))
-            for m in range(6):
-                o = v("ot", 768 * (m // 3) + m % 3, 768 * (m // 3) + 768, 4)
-                ts(o, o, v("sp%d" % (p - 1), 32 * m + 31, 32 * m + 32), thr, A.mult, A.is_lt)
-            count(0)
-            count(1)
-            count(2)
+            for m in range(3):
+                act(hot(m), hot(m), F.Identity, scale=v("rm", m, m + 1))
+            for m in range(3, 9):
+                ts(hot(m), hot(m), v("sp%d" % (p - 1), 48 * m + 47, 48 * m + 48), thr, A.mult, A.is_lt)
+        count(1, True, False)
+        count(2, False, False)
+        count(0, False, True)
         fill()
-        tt(v("wn"), v("enc"), bank(6, 192), A.subtract)
-        act(v("g2", 0, 2 * H, 2), gat(v("wn"), v(ho, 0, 9)))
-        cp(v("g1"), gat(v("wn"), v(ho, 10, 19)))
-        tt(v("g2", 1, 2 * H, 2), gat(v("wn"), v(ho, 20, 29)), v("g1"), A.max)
-        scan(v("sp%d" % p), v("c32"), v("g2"), A.add)
+        for k in range(3):
+            tt(v("wn", 64 * k, 64 * k + 64), v("enc", 64 * k, 64 * k + 64), v("ps", 3072 + 64 * k, 3136 + 64 * k), A.subtract)
+        for q, k, a, b in ((act, 0, 0, 4), (cp, 1, 0, 4), (cp, 2, 0, 4), (act, 0, 4, 9), (act, 1, 4, 9), (cp, 2, 4, 9)):
+            q(v("g3", 48 * a + k, 48 * b, 3), gat(v("wn", 0, 64 * k + 64), v(ho, 10 * k + a, 10 * k + b)))
+        scan(v(sp, 0, 192), v("c48", 0, 192), v("g3", 0, 192), A.add)
+        scan(v(sp, 192, 432), v("c48", 192, 432), v("g3", 192, 432), A.add)
         if p < 2:
-            ts(v("rm"), v("sp%d" % p, 31, 2 * H, 32), thr, None, A.is_lt)
+            ts(v("rm", 0, 3), v(sp, 47, 144, 48), thr, None, A.is_lt)
 
     def keep(p):
-        a = v("sp%d" % p, 31, 2 * H, 32)
+        a = v("sp%d" % p, 47, 3 * H, 48)
         ts(v("q9"), a, thr, 16384.0 / (p + 1), A.is_gt, A.mult)
         if p == 0:
             ts(v("dm"), v("dm0"), v("dsc"), None, A.add)
@@ -318,7 +317,7 @@ def rank_program(g, core, T, topo):
         peel(t, 0, fill0)
         peel(t, 1, lambda: keep(0))
         peel(t, 2, lambda: keep(1))
-        tt(v("en"), v("sp2", 31, 2 * H, 32), v("ac1"), A.max)
+        tt(v("en"), v("sp2", 47, 3 * H, 48), v("ac1"), A.max)
         ts(v("li", 0, 9), v("en"), 1023, None, A.bitwise_and)
         tt(v("xy", 0, 9), v("s01"), v("li", 0, 9), A.subtract)
         tt(v("xy", 9, 18), v("s12"), v("li", 0, 9), A.subtract)
@@ -334,7 +333,7 @@ def rank_program(g, core, T, topo):
         act(v("tw2"), v("tw", 0, 256))
         act(v("iv", 0, 960, 3), v("tw", 256, 576), scale=-1.0)
         if t == 0:
-            keys(1, "hr", setup_f)
+            keys(1, "hr", setup_f, lambda: ts(v("sc12"), v("sc4"), 3.0, None, A.mult))
             act(v("c4"), v("sg4"), scale=256.0)
             cp(v("ho3"), v("hr"))
         if t == 1:
@@ -350,17 +349,21 @@ def rank_program(g, core, T, topo):
         cp(v("ga", 0, H), gat(v(ow, 0, 192), v(ll, 10, 19)))
         scan(v("gb"), v("c4", 0, 2 * H), v("ga"), A.mult)
         ts(v("oab"), v("gb", 3, 2 * H, 4), v("sc4"), v("tm4"), A.mult, A.add)
+        ts(v("oab3"), v("gb", 3, 2 * H, 4), v("sc12"), v("tm12"), A.mult, A.add)
         for a, b in ((16, 30), (30, 36)):
             for s in range(2):
                 act(v("iv", 48 * (a - 16) + 1 + s, 48 * (b - 16), 3), gat(v("tw"), v("oab", 36 * s + a, 36 * s + b)))
         act(v("ra"), gat(v(ow, 0, 192), v(rlist[t])))
-        tt(v("t1"), gat(v("tw"), v("oab", 0, 16)), v("tw2"), A.subtract)
-        ts(v("oab3"), v("gb", 3, 2 * H, 4), v("sc12"), v("tm12"), A.mult, A.add)
-        tt(v("n3", 2, 768, 3), gat(v("tw"), v("oab", 36, 52)), v("t1"), A.add)
+        for a in (0, 8):
+            tt(v("t1", 16 * a, 16 * a + 128), gat(v("tw"), v("oab", a, a + 8)), v("tw2", 16 * a, 16 * a + 128), A.subtract)
+        for a in (0, 8):
+            tt(v("n3", 48 * a + 2, 48 * a + 384, 3), gat(v("tw"), v("oab", 36 + a, 44 + a)), v("t1", 16 * a, 16 * a + 128), A.add)
         scan(v("n3", 768, 1440), v("c3"), v("iv", 0, 672), A.mult, A.add)
         scan(v("n3", 1440, 1728), v("c3", 0, 288), v("iv", 672, 960), A.mult, A.add)
-        tt(v("t2"), gat(v("n3"), v("oab3", 0, 36)), v("tw", 0, 576), A.add)
-        tt(v("zt"), gat(v("n3"), v("oab3", 36, 72)), v("t2"), A.add)
+        for a, b in ((0, 22), (22, 36)):
+            tt(v("t2", 16 * a, 16 * b), gat(v("n3"), v("oab3", a, b)), v("tw", 16 * a, 16 * b), A.add)
+        for a, b in ((0, 22), (22, 36)):
+            tt(v("zt", 16 * a, 16 * b), gat(v("n3"), v("oab3", 36 + a, 36 + b)), v("t2", 16 * a, 16 * b), A.add)
         quant(v("zq"), v("zs"), v("zt"))
         for b in range(4):
             mm(bank(4 + b, H), *eb(b), v("zq"), v("zs"))
@@ -371,11 +374,13 @@ def rank_program(g, core, T, topo):
                 act(v("ew", b, 576, 4), bank(4 + b, H), scale=2.0 ** -6)
             else:
                 ts(v("ew", b, 576, 4), bank(4 + b, H), 2.0 ** -6, None, A.mult)
-        act(v("f0", 192, 576), gat(v("ew"), v("ord", 12, 36)))
-        cp(v("f0", 0, 192), gat(v("ew"), v("ord", 0, 12)))
-        tt(v("f1", 0, 192), gat(v("ew"), v("ord", 40, 52)), v("f0", 0, 192), A.add)
-        tt(v("f1", 192, 576), gat(v("ew"), v("ord", 52, 76)), v("f0", 192, 576), A.add)
-        tt(v("ft"), gat(v("ew"), v("ord", 80, 116)), v("f1"), A.add)
+        for a, b in ((8, 20), (20, 36)):
+            act(v("f0", 16 * a, 16 * b), gat(v("ew"), v("ord", a, b)))
+        cp(v("f0", 0, 128), gat(v("ew"), v("ord", 0, 8)))
+        for a, b in ((0, 8), (8, 20), (20, 36)):
+            tt(v("f1", 16 * a, 16 * b), gat(v("ew"), v("ord", 40 + a, 40 + b)), v("f0", 16 * a, 16 * b), A.add)
+        for a, b in ((0, 20), (20, 36)):
+            tt(v("ft", 16 * a, 16 * b), gat(v("ew"), v("ord", 80 + a, 80 + b)), v("f1", 16 * a, 16 * b), A.add)
         quant(v("fq"), v("fs"), v("ft"))
         for b in range(4):
             mm(bank(b, H), v("wq", 128 * b, 128 * b + 128), v("wsc", 128 * b, 128 * b + 128), v("fq"), v("fs"), False, True)

from concourse.mybir import dt, AluOpType as A, ActivationFunctionType as F, AxisListType as AX

H = 144
BIG = float(2 ** 20)
CQ, BF, F32, I32, U16, U8 = "float8_e4m3fn_x4", "bfloat16", "float32", "int32", "uint16", "uint8"
COLS = "pw bigp sc4 tm4 sc12 tm12 dsc nq thr".split()

SCRATCH = {"ps": ("psum", [128, 4096], F32)}
for _names, _n, _t in [
    ("xa xb", 576, BF), ("ub vb", 512, BF), ("hci", 4, I32), ("hcf", 4, F32),
    ("wq", 512, CQ), ("wsc", 512, U8), ("uq vq kwq boq", 128, CQ), ("us vs kws bos", 128, U8),
    ("kw bo", 512, BF), ("eye", 516, BF), ("c64", 128, BF), ("eq", 512, CQ), ("es", 512, U8),
    ("pidx", 1, I32), ("pint", 4, I32), ("pf", 4, F32), ("grp", 128, BF), ("jm c16a c16", H, F32), ("c48", 3 * H, F32),
    ("jm4 sg4 c4", 480, BF), ("c3", 672, BF), ("d16", 16, F32), ("d4", 4, F32),
    ("col", len(COLS), F32), ("cell", 192, BF), ("enc", 192, F32), ("dm0 dm", 9, F32), ("ids", H, BF),
    ("bt", 576, BF), ("btq", H, CQ), ("bts", H, U8), ("ks", H, F32), ("xi hb li", 30, I32), ("hg hr", 30, F32),
    ("ot", 2304, BF), ("otq", 576, CQ), ("ots", 576, U8), ("wn", 192, F32), ("g3 sp0 sp1 sp2", 3 * H, F32),
    ("s01 s12 rm q9 z9 ac0 ac1", 9, F32), ("en", 9, I32), ("xy", 18, F32),
    ("tw ew", 580, BF), ("tw2", 256, BF), ("iv", 960, BF), ("n3", 1740, BF), ("t1", 256, F32), ("t2 f1", 576, F32),
    ("zt f0 ft xn", 576, BF), ("zq fq", H, CQ), ("zs fs", H, U8), ("ga gb", 2 * H, BF), ("oab oab3", 72, U16),
    ("ra rb", 480, BF), ("ord", 120, U16), ("ya yb", H, F32),
    ("xq0 xq1 xq2 xq3 xq4", H, CQ), ("xs0 xs1 xs2 xs3 xs4", H, U8),
    ("ho0 ho1 ho2 ho3", 30, U16),
    ("lq0 lq1 lq2", H, CQ), ("ls0 ls1 ls2", H, U8), ("ll0 ll1 ll2 sl0 sl1 sl2", 30, U16), ("ow0 ow1 ow2", 336, BF),
]:
    for _x in _names.split():
        SCRATCH[_x] = ("sbuf", [128, _n], _t)

SEMAPHORES = ["nV", "nS", "nP", "nG", "sent", "stY", "stS"] + ["ld%d" % i for i in range(8)] + \
             ["ac%d" % i for i in range(3)] + ["al%d" % i for i in range(3)]


def rank_program(g, core, T, topo):
    rank = T.rank_of(core)
    if rank is None:
        return
    nxt = T.cores[(rank + 1) % len(T.cores)]
    rid, pid = topo.addr(nxt, core)
    mask = topo.mask(core, nxt)
    neng = len(topo.engines(core, nxt))
    Q = {"V": g.vector, "S": g.scalar, "P": g.tensor, "G": g, "Y": g.sync}
    ops = []

    def v(name, a=0, b=None, s=1):
        if name in COLS:
            return ("col", COLS.index(name), COLS.index(name) + 1, 1)
        return (name, a, SCRATCH[name][1][1] if b is None else b, s)

    def ap(x):
        if isinstance(x, tuple):
            return T[x[0]][:, x[1]:x[2]] if x[3] == 1 else T[x[0]][:, x[1]:x[2]:x[3]]
        return x

    def bank(b, n):
        return v("ps", 512 * b, 512 * b + n)

    def add(q, fn, reads, writes, sem=None, inc=0):
        ops.append({"q": q, "fn": fn, "r": [x for x in reads if isinstance(x, tuple)], "w": list(writes), "sem": sem, "inc": inc})

    def src(x):
        if isinstance(x, list):
            return ap(x[1]).indirect(ap(x[2]))
        return ap(x)

    def rd(x):
        return [x[1], x[2]] if isinstance(x, list) else [x]

    def gat(win, off):
        return ["gather", win, off]

    def ts(out, in0, s1, s2, o0, o1=None):
        if o1 is None:
            add("V", lambda: g.vector.tensor_scalar(ap(out), src(in0), ap(s1), None, o0), rd(in0) + [s1], [out])
        else:
            add("V", lambda: g.vector.tensor_scalar(ap(out), src(in0), ap(s1), ap(s2), o0, o1), rd(in0) + [s1, s2], [out])

    def tt(out, in0, in1, o):
        add("V", lambda: g.vector.tensor_tensor(ap(out), src(in0), ap(in1), o), rd(in0) + [in1], [out])

    def cp(out, in_):
        add("V", lambda: g.vector.tensor_copy(ap(out), src(in_)), rd(in_), [out])

    def scatter(win, off, in_):
        add("V", lambda: g.vector.tensor_copy(ap(win).indirect(ap(off)), ap(in_)), [off, in_], [win])

    def ms(out, c):
        add("V", lambda: g.vector.memset(ap(out), c), [], [out])

    def scan(out, d0, d1, o0, o1=A.max):
        add("V", lambda: g.vector.tensor_tensor_scan(ap(out), ap(d0), ap(d1), 0.0, o0, o1), [d0, d1], [out])

    def prod(out, in_):
        add("V", lambda: g.vector.tensor_reduce(ap(out), ap(in_), AX.X, A.mult), [in_], [out])

    def act(out, in_, f=F.Copy, scale=1.0, bias=None):
        if bias is None:
            add("S", lambda: g.scalar.activation(ap(out), src(in_), f, scale=ap(scale)), rd(in_) + [scale], [out])
        else:
            add("S", lambda: g.scalar.activation(ap(out), src(in_), f, bias=ap(bias), scale=ap(scale)), rd(in_) + [scale, bias], [out])

    def quant(c, s, in_):
        add("V", lambda: g.vector.quantize_mx(ap(c), ap(s), ap(in_)), [in_], [c, s])

    def mm(out, lc, ls, rc, rs, start=True, stop=True):
        add("P", lambda: g.tensor.matmul_mx(ap(out), ap(lc), ap(ls), ap(rc), ap(rs), start, stop), [lc, ls, rc, rs], [out])

    def iota(out, pat, base, ch=0):
        if SCRATCH[out[0]][2] == I32:
            add("G", lambda: g.iota(ap(out), pat, base, ch), [], [out])
        else:
            add("G", lambda: g.iota(ap(out), pat, base, ch, allow_small_or_imprecise_dtypes=True), [], [out])

    def fillg(out, c):
        iota(out, [[0, len(range(out[1], out[2], out[3]))]], c)

    def load(q, out, out_ap, in_ap, sem):
        add(q, lambda: Q[q].dma_start(out_ap, in_ap), [], [out], sem, 16)

    def store(q, out_ap, in_, in_ap):
        add(q, lambda: Q[q].dma_start(out_ap, in_ap), [in_], [], "st" + q, 16)

    def send(out_ap, in_, in_ap, sem):
        add("G", lambda: g.remote_dma(out_ap, in_ap, T.sem[sem], T.sem.sent, pid, rid, mask), [in_], [], "sent", 0)

    def arrive(outs, sem, n):
        add(None, None, [], outs, sem, n)

    def u8(name):
        return T[name][:].bitcast(dt.uint8)

    def xq(i):
        return v("xq%d" % i), v("xs%d" % i)

    def eb(b):
        return v("eq", 128 * b, 128 * b + 128), v("es", 128 * b, 128 * b + 128)

    pi, pg, pt, pq = v("pf", 0, 1), v("pf", 1, 2), v("pf", 2, 3), v("pf", 3, 4)
    bigp, thr = v("bigp"), v("thr")

    load("Y", v("xa"), T.xa[:], T.x[:, 0:576], "ld0")
    load("S", v("ub"), T.ub[:], T.u[:], "ld1")
    load("Y", v("xb"), T.xb[:], T.x[:, 576:1152], "ld3")
    load("S", v("hci", 0, 3), T.hci[:, 0:3], T.hc[:], "ld2")
    load("Y", v("wq"), u8("wq"), T.wc[:], "ld4")
    load("Y", v("wsc"), T.wsc[:], T.ws[:], "ld5")
    load("Y", v("vb"), T.vb[:], T.v[:], "ld6")
    for t in range(3):
        arrive([v("lq%d" % t), v("ls%d" % t)], "ac%d" % t, 2 * neng)
        arrive([v("ll%d" % t)], "al%d" % t, neng)

    iota(v("pidx"), [[0, 1]], 0, 1)
    iota(v("jm"), [[0, 9], [1, 16]], 0)
    iota(v("grp"), [[1, 8], [0, 16]], 0)
    ms(v("c64"), 64.0)
    ms(v("eye"), 0.0)
    add("G", lambda: g.affine_select(ap(v("eye", 3, 515, 4)), ap(v("c64")), [[-1, 128]], A.is_equal, 0.0, 0, 1), [v("c64")], [v("eye", 3, 515, 4)])
    iota(v("cell"), [[1, 192]], 0)
    fillg(v("xi"), 0)
    fillg(v("ot", 3, 2304, 4), 0)
    ts(v("pint", 0, 1), v("pidx"), 15, None, A.bitwise_and)
    ts(v("pint", 1, 2), v("pidx"), 4, None, A.logical_shift_right)
    ts(v("pint", 2, 3), v("pidx"), 3, None, A.bitwise_and)
    ts(v("pint", 3, 4), v("pidx"), 2, 3, A.logical_shift_right, A.bitwise_and)
    ms(v("kw"), 0.0)
    cp(v("pf"), v("pint"))
    ms(v("bt"), 0.0)
    ts(v("d16"), v("jm", 0, 16), pi, 1.0, A.is_lt, A.add)
    ts(bigp, pi, -BIG, 15 * BIG, A.mult, A.add)
    ts(v("c16a"), v("jm"), pi, 31.0 / 32, A.is_gt, A.subtract)
    ts(v("bo", 0, 512, 4), v("grp"), pg, 4096.0, A.is_equal, A.mult)
    prod(v("pw"), v("d16"))
    act(v("c16"), v("c16a"), scale=32 * BIG)
    for t in range(1, 4):
        act(v("bo", t, 512, 4), v("bo", 0, 512, 4))
    act(v("c48", 0, 3 * H, 3), v("c16a"), scale=32 * BIG)
    act(v("c48", 1, 3 * H, 3), v("c16a"), scale=0.0)
    act(v("c48", 2, 3 * H, 3), v("c16a"), scale=0.0)
    quant(*eb(0), v("eye", 3, 515))
    quant(*eb(1), v("eye", 2, 514))
    ts(v("kw", 0, 512, 4), v("grp"), pg, v("pw"), A.is_equal, A.mult)
    quant(*eb(2), v("eye", 1, 513))
    quant(*eb(3), v("eye", 0, 512))
    quant(v("kwq"), v("kws"), v("kw"))
    quant(*xq(0), v("xa"))
    quant(v("uq"), v("us"), v("ub"))

    def setup_b():
        quant(*xq(1), v("xb"))
        cp(v("hcf", 0, 3), v("hci", 0, 3))

    def setup_c():
        quant(v("boq"), v("bos"), v("bo"))
        ts(thr, pi, -BIG, -BIG, A.mult, A.add)
        ts(v("dsc"), pi, 1 - BIG, -BIG, A.mult, A.add)

    def setup_g():
        iota(v("enc"), [[64 - 1024, 3], [1, 64]], 3072 + 4096 - 2 ** 24)
        iota(v("dm0"), [[16, 9]], 192)
        fillg(v("li"), 0)
        iota(v("jm4"), [[0, 120], [1, 4]], 0)
        iota(v("ids"), [[4, H]], 4)
        fillg(v("ow0"), 580)
        fillg(v("tw", 576, 580), 0)
        fillg(v("ew", 576, 580), 0)
        fillg(v("n3", 1728, 1740), 0)
        fillg(v("n3", 0, 768), 0)
        fillg(v("c3", 0, 672, 3), 0)

    def setup_f():
        ts(v("nq"), pq, -1.0, -0.5, A.mult, A.add)
        ts(v("d4"), v("jm4", 0, 4), pq, 2.0 ** -8, A.is_le, A.max)
        ts(v("tm4"), pt, -4.0, None, A.add)
        ts(v("tm12"), pt, 3.0, -10.0, A.mult, A.add)
        ms(v("c3", 1, 672, 3), 1.0)
        prod(v("sc4"), v("d4"))
        act(v("sg4"), v("jm4"), F.Sign, bias=v("nq"))
        ms(v("c3", 2, 672, 3), 1.0)

    def keys(xi_, hg, fill1=None, fill2=None):
        mm(bank(4, H), v("uq"), v("us"), *xq(xi_))
        if fill1:
            fill1()
        ts(v("bt", 0, 576, 4), bank(4, H), 0.0, None, A.is_gt)
        quant(v("btq"), v("bts"), v("bt"))
        mm(bank(5, H), v("kwq"), v("kws"), v("btq"), v("bts"))
        if fill2:
            fill2()
        scan(v("ks"), v("c16"), bank(5, H), A.add)
        for k in range(3):
            ts(v("xi", 10 * k, 10 * k + 9), v("ks", 15, H, 16), bigp, v("hcf", k, k + 1), A.subtract, A.mult)
        for k in range(3):
            ts(v("hb", 10 * k, 10 * k + 10), v("xi", 10 * k, 10 * k + 10), 8, 63, A.logical_shift_right, A.bitwise_and)
        for k in range(3):
            ts(v(hg, 10 * k, 10 * k + 10), v("hb", 10 * k, 10 * k + 10), 64.0 * k, None, A.add)

    def hcol(k, m):
        return v("hg", 10 * k + m, 10 * k + m + 1)

    def hlist(k):
        return v("hg", 10 * k, 10 * k + 9)

    def count(j, first, last):
        c, s = v("otq", 192 * j, 192 * j + 192), v("ots", 192 * j, 192 * j + 192)
        quant(c, s, v("ot", 768 * j, 768 * j + 768))
        mm(bank(6, 192), v("boq"), v("bos"), c, s, first, last)

    def hot(m, k=None):
        a = 768 * (m // 3) + m % 3
        return v("ot", a, 768 * (m // 3) + 768, 4) if k is None else v("ot", a + 256 * k, a + 256 * k + 253, 4)

    def peel(t, p, fill):
        ho, sp = "ho%d" % t, "sp%d" % p
        if p == 0:
            for k in range(3):
                for m in range(3):
                    act(hot(m, k), v("cell", 64 * k, 64 * k + 64), F.Abs, scale=-1.0, bias=hcol(k, m))
            for m in range(3):
                act(hot(m), hot(m), F.Relu, scale=-1.0, bias=1.0)
            for j in (1, 2):
                for k in range(3):
                    for m in range(3 * j, 3 * j + 3):
                        ts(hot(m, k), v("cell", 64 * k, 64 * k + 64), hcol(k, m), None, A.is_equal)
        else:
            for m in range(3):
                act(hot(m), hot(m), F.Identity, scale=v("rm", m, m + 1))
            for m in range(3, 9):
                ts(hot(m), hot(m), v("sp%d" % (p - 1), 48 * m + 47, 48 * m + 48), thr, A.mult, A.is_lt)
        count(1, True, False)
        count(2, False, False)
        count(0, False, True)
        fill()
        for k in range(3):
            tt(v("wn", 64 * k, 64 * k + 64), v("enc", 64 * k, 64 * k + 64), v("ps", 3072 + 64 * k, 3136 + 64 * k), A.subtract)
        for q, k, a, b in ((act, 0, 0, 4), (cp, 1, 0, 4), (cp, 2, 0, 4), (act, 0, 4, 9), (act, 1, 4, 9), (cp, 2, 4, 9)):
            q(v("g3", 48 * a + k, 48 * b, 3), gat(v("wn", 0, 64 * k + 64), v(ho, 10 * k + a, 10 * k + b)))
        scan(v(sp, 0, 192), v("c48", 0, 192), v("g3", 0, 192), A.add)
        scan(v(sp, 192, 432), v("c48", 192, 432), v("g3", 192, 432), A.add)
        if p < 2:
            ts(v("rm", 0, 3), v(sp, 47, 144, 48), thr, None, A.is_lt)

    def keep(p):
        a = v("sp%d" % p, 47, 3 * H, 48)
        ts(v("q9"), a, thr, 16384.0 / (p + 1), A.is_gt, A.mult)
        if p == 0:
            ts(v("dm"), v("dm0"), v("dsc"), None, A.add)
        tt(v("z9"), v("q9"), a, A.add)
        tt(v("ac%d" % p), v("z9"), v("dm") if p == 0 else v("ac0"), A.max)

    def finish_half(i, lo, ybuf, b):
        mm(bank(b, H), v("vq"), v("vs"), *xq(i))
        store("Y", T.oc[:, 4 * lo:4 * lo + 4 * H], v("xq%d" % i), u8("xq%d" % i))
        for k in range(4):
            store("S" if i == 4 else "Y", T.osc[4 * k:4 * k + 4, lo:lo + H], v("xs%d" % i), T["xs%d" % i][32 * k:32 * k + 4, :])
        if i == 4:
            cp(v(ybuf), bank(b, H))
        else:
            act(v(ybuf), bank(b, H))
        store("Y", T.y[:, lo:lo + H], v(ybuf), T[ybuf][:])

    writers, readers, rlist = [0, 2, 3], [1, 0, 2], ["ho3", "ho0", "ho1"]
    for t in range(3):
        w = writers[t]
        send(u8("lq%d" % t), v("xq%d" % w), u8("xq%d" % w), "ac%d" % t)
        send(T["ls%d" % t][:], v("xs%d" % w), T["xs%d" % w][:], "ac%d" % t)
        if t == 0:
            setup_g()
            keys(w, "hg", setup_b, setup_c)
        else:
            fillg(v("ow%d" % t), 580)
            keys(w, "hg")

        def fill0():
            cp(v("ho%d" % t), v("hg"))
            tt(v("s01"), hlist(0), hlist(1), A.add)
            tt(v("s12"), hlist(1), hlist(2), A.add)

        peel(t, 0, fill0)
        peel(t, 1, lambda: keep(0))
        peel(t, 2, lambda: keep(1))
        tt(v("en"), v("sp2", 47, 3 * H, 48), v("ac1"), A.max)
        ts(v("li", 0, 9), v("en"), 1023, None, A.bitwise_and)
        tt(v("xy", 0, 9), v("s01"), v("li", 0, 9), A.subtract)
        tt(v("xy", 9, 18), v("s12"), v("li", 0, 9), A.subtract)
        tt(v("li", 10, 19), v("xy", 0, 9), hlist(0), A.max)
        tt(v("li", 20, 29), v("xy", 9, 18), hlist(2), A.min)
        cp(v("sl%d" % t), v("li"))
        send(T["ll%d" % t][:], v("sl%d" % t), T["sl%d" % t][:], "al%d" % t)

        for b in range(4):
            mm(bank(b, H), *eb(b), v("lq%d" % t), v("ls%d" % t))
        for b in range(4):
            act(v("tw", b, 576, 4), bank(b, H), scale=2.0 ** -6)
        act(v("tw2"), v("tw", 0, 256))
        act(v("iv", 0, 960, 3), v("tw", 256, 576), scale=-1.0)
        if t == 0:
            keys(1, "hr", setup_f, lambda: ts(v("sc12"), v("sc4"), 3.0, None, A.mult))
            act(v("c4"), v("sg4"), scale=256.0)
            cp(v("ho3"), v("hr"))
        if t == 1:
            quant(v("vq"), v("vs"), v("vb"))
        if t == 2:
            finish_half(3, 0, "ya", 7)
        for b in range(4):
            mm(bank(b, H), *eb(b), *xq(readers[t]), True, False)

        ll, ow = "ll%d" % t, "ow%d" % t
        scatter(v(ow), v(ll, 0, 9), v("ids"))
        act(v("ga", H, 2 * H), gat(v(ow, 0, 192), v(ll, 20, 29)))
        cp(v("ga", 0, H), gat(v(ow, 0, 192), v(ll, 10, 19)))
        scan(v("gb"), v("c4", 0, 2 * H), v("ga"), A.mult)
        ts(v("oab"), v("gb", 3, 2 * H, 4), v("sc4"), v("tm4"), A.mult, A.add)
        ts(v("oab3"), v("gb", 3, 2 * H, 4), v("sc12"), v("tm12"), A.mult, A.add)
        for a, b in ((16, 30), (30, 36)):
            for s in range(2):
                act(v("iv", 48 * (a - 16) + 1 + s, 48 * (b - 16), 3), gat(v("tw"), v("oab", 36 * s + a, 36 * s + b)))
        act(v("ra"), gat(v(ow, 0, 192), v(rlist[t])))
        for a in (0, 8):
            tt(v("t1", 16 * a, 16 * a + 128), gat(v("tw"), v("oab", a, a + 8)), v("tw2", 16 * a, 16 * a + 128), A.subtract)
        for a in (0, 8):
            tt(v("n3", 48 * a + 2, 48 * a + 384, 3), gat(v("tw"), v("oab", 36 + a, 44 + a)), v("t1", 16 * a, 16 * a + 128), A.add)
        scan(v("n3", 768, 1440), v("c3"), v("iv", 0, 672), A.mult, A.add)
        scan(v("n3", 1440, 1728), v("c3", 0, 288), v("iv", 672, 960), A.mult, A.add)
        for a, b in ((0, 22), (22, 36)):
            tt(v("t2", 16 * a, 16 * b), gat(v("n3"), v("oab3", a, b)), v("tw", 16 * a, 16 * b), A.add)
        for a, b in ((0, 22), (22, 36)):
            tt(v("zt", 16 * a, 16 * b), gat(v("n3"), v("oab3", 36 + a, 36 + b)), v("t2", 16 * a, 16 * b), A.add)
        quant(v("zq"), v("zs"), v("zt"))
        for b in range(4):
            mm(bank(4 + b, H), *eb(b), v("zq"), v("zs"))
        scan(v("rb"), v("c4"), v("ra"), A.mult)
        ts(v("ord"), v("rb", 3, 480, 4), v("sc4"), v("tm4"), A.mult, A.add)
        for b in range(4):
            if b % 2 == 0:
                act(v("ew", b, 576, 4), bank(4 + b, H), scale=2.0 ** -6)
            else:
                ts(v("ew", b, 576, 4), bank(4 + b, H), 2.0 ** -6, None, A.mult)
        for a, b in ((8, 20), (20, 36)):
            act(v("f0", 16 * a, 16 * b), gat(v("ew"), v("ord", a, b)))
        cp(v("f0", 0, 128), gat(v("ew"), v("ord", 0, 8)))
        for a, b in ((0, 8), (8, 20), (20, 36)):
            tt(v("f1", 16 * a, 16 * b), gat(v("ew"), v("ord", 40 + a, 40 + b)), v("f0", 16 * a, 16 * b), A.add)
        for a, b in ((0, 20), (20, 36)):
            tt(v("ft", 16 * a, 16 * b), gat(v("ew"), v("ord", 80 + a, 80 + b)), v("f1", 16 * a, 16 * b), A.add)
        quant(v("fq"), v("fs"), v("ft"))
        for b in range(4):
            mm(bank(b, H), v("wq", 128 * b, 128 * b + 128), v("wsc", 128 * b, 128 * b + 128), v("fq"), v("fs"), False, True)
        for b in range(4):
            if b % 2 == 0:
                act(v("xn", b, 576, 4), bank(b, H), scale=2.0 ** -6)
            else:
                ts(v("xn", b, 576, 4), bank(b, H), 2.0 ** -6, None, A.mult)
        quant(*xq(2 + t), v("xn"))
    finish_half(4, H, "yb", 7)

    def cols(x):
        if x[0] == "ps":
            return {x[1] // 512}
        return set(range(x[1], x[2], x[3]))

    seen = {}
    clock = {q: {} for q in Q}
    seq = {q: 0 for q in Q}
    for i, o in enumerate(ops):
        q = o["q"]
        deps = set()
        acc = [(x[0], cols(x), False) for x in o["r"]] + [(x[0], cols(x), True) for x in o["w"]]
        for name, cs, wr in acc:
            for j, cj, wj in seen.get(name, []):
                qj = ops[j]["q"]
                if name == "ps":
                    if qj == q and (q == "P" or not (wr or wj)):
                        continue
                elif not (wr or wj):
                    continue
                if cs & cj:
                    deps.add(j)
        for name, cs, wr in acc:
            seen.setdefault(name, []).append((i, cs, wr))
        if o["sem"] is None:
            seq[q] += 1
            o["key"], o["pos"] = q, seq[q]
        else:
            o["key"], o["pos"] = ("a", i), 1
        o["waits"] = []
        if q is not None:
            ck = clock[q]
            for j in sorted(deps, reverse=True):
                d = ops[j]
                if ck.get(d["key"], 0) >= d["pos"]:
                    continue
                o["waits"].append(j)
                d["sig"] = True
                for kk, vv in d["clock"].items():
                    if ck.get(kk, 0) < vv:
                        ck[kk] = vv
                ck[d["key"]] = max(ck.get(d["key"], 0), d["pos"])
            o["clock"] = dict(ck)
        else:
            o["clock"] = {}
    n = {q: 0 for q in Q}
    total = {}
    for o in ops:
        if o["sem"] is None:
            if o.get("sig"):
                n[o["q"]] += 1
                o["val"] = n[o["q"]]
        else:
            o["val"] = o["inc"]
    for o in ops:
        q = o["q"]
        if q is None:
            continue
        for j in o["waits"]:
            d = ops[j]
            Q[q].wait_ge(T.sem[d["sem"] or "n" + d["q"]], d["val"])
        ins = o["fn"]()
        if o["sem"] is None:
            if o.get("sig"):
                ins.then_inc(T.sem["n" + q], 1)
        elif o["inc"]:
            ins.then_inc(T.sem[o["sem"]], o["inc"])
            total[o["sem"]] = total.get(o["sem"], 0) + o["inc"]
    g.wait_ge(T.sem.sent, 9 * neng)
    g.sync.wait_ge(T.sem.stY, total["stY"])
    g.scalar.wait_ge(T.sem.stS, total["stS"])
